import numpy as np
import ml_dtypes


def mxq(x, axis, fmt="e4m3"):
    dtype, down = {"e4m3": (ml_dtypes.float8_e4m3fn, 7), "e5m2": (ml_dtypes.float8_e5m2, 14)}[fmt]
    v = np.moveaxis(np.asarray(x, np.float32).astype(ml_dtypes.bfloat16).astype(np.float64), axis, -1)
    blocks = v.reshape(v.shape[:-1] + (-1, 32))
    amax = np.abs(blocks).max(-1, keepdims=True)
    byte = np.maximum(np.where(amax > 0, np.frexp(amax)[1] - 1 + 127, 0) - down, 1)
    scale = np.exp2(byte - 127.0)
    codes = (blocks / scale).astype(np.float32).astype(dtype).astype(np.float64)
    return np.moveaxis((codes * scale).reshape(v.shape), -1, axis)


WIDE = False


def mx_kscale(k):
    if not WIDE:
        return np.ones(k)
    levels = np.array([10, -10, 5, -5, 0])
    if k % 512:
        return np.exp2(np.random.permutation(np.resize(levels, k // 32))).repeat(32)
    a = np.empty((k // 512, 16))
    for p in range(k // 512):
        a[p, :8] = np.random.permutation(np.resize(levels, 8))
        for g in range(8):
            far = levels[np.abs(levels - a[p, g]) >= 10]
            a[p, g + 8] = far[np.random.randint(len(far))]
    return np.exp2(a.ravel()).repeat(32)


def f64(x):
    return np.asarray(x).astype(np.float64)


def striped(idx):
    return np.tile(idx.reshape(-1, 16).T, (8, 1)).astype(np.uint16)


def unstriped(offs):
    return offs[:16].T.reshape(-1).astype(np.int64)


E2M1 = np.array([0.0, 0.5, 1.0, 1.5, 2.0, 3.0, 4.0, 6.0, -0.0, -0.5, -1.0, -1.5, -2.0, -3.0, -4.0, -6.0])


def pack_weight(w, fmt):
    k, n = w.shape
    w = f64(np.asarray(w, np.float32).astype(ml_dtypes.bfloat16)).reshape(k // 32, 32, n)
    amax = np.abs(w).max(1)
    if fmt == "e4m3":
        byte = np.frexp(amax)[1] - 1 + 127 - 7
    else:
        mant, ex = np.frexp(amax / 6.0)
        byte = np.where(mant > 0.5, ex, ex - 1) + 127
    byte = np.clip(np.where(amax > 0, byte, 1), 1, 254)
    scaled = (w * np.exp2(127.0 - byte)[:, None, :]).reshape(k, n).astype(np.float32)
    by_word = np.ascontiguousarray(scaled.reshape(k // 512, 128, 4, n).transpose(0, 1, 3, 2))
    if fmt == "e4m3":
        words = by_word.astype(ml_dtypes.float8_e4m3fn).view(np.uint8)
    else:
        c = by_word.astype(ml_dtypes.float4_e2m1fn).view(np.uint8) & 0xF
        words = (c[..., 0::2] | (c[..., 1::2] << 4)).reshape(k // 512, 128, 2 * n)
    return np.ascontiguousarray(words), np.ascontiguousarray(byte.astype(np.uint8).reshape(k // 512, 16, n))


def unpack_weight(words, scales, fmt):
    g, _, n = scales.shape
    words = np.ascontiguousarray(words).reshape(g, 128, n, -1)
    if fmt == "e4m3":
        vals = words.view(ml_dtypes.float8_e4m3fn).astype(np.float64)
    else:
        nib = np.empty((g, 128, n, 4), np.uint8)
        nib[..., 0::2] = words & 0xF
        nib[..., 1::2] = words >> 4
        vals = E2M1[nib]
    vals = vals * np.repeat(np.exp2(scales.astype(np.float64) - 127.0), 8, axis=1)[..., None]
    return vals.transpose(0, 1, 3, 2).reshape(g * 512, n)


def gelu(v):
    return 0.5 * v * (1.0 + np.tanh(np.sqrt(2.0 / np.pi) * (v + 0.044715 * v**3)))


K, H, N, T, S, T2 = 1024, 512, 512, 4096, 1024, 2048

def setup_inputs():
    n = np.random.standard_normal
    s = mx_kscale(K)[:, None]
    u = mx_kscale(H)[:, None]
    tab_words, tab_scales = pack_weight(n((K, T)) * s, "e4m3")
    b4_words, b4_scales = pack_weight(n((K, H)) / np.sqrt(K) / s * u.T, "e2m1")
    d8_words, d8_scales = pack_weight(n((K, N)) / np.sqrt(K) / s, "e4m3")
    return {
        "tab_words": tab_words, "tab_scales": tab_scales,
        "offs": striped(np.random.permutation(T)[:S]),
        "offs2": striped(np.random.permutation(T)[:S]),
        "offs3": striped(np.random.permutation(T2)[:S]),
        "wa": (n((K, H)) / np.sqrt(K) / s * u.T).astype(np.float32),
        "bw": (0.5 * n(H) * u[:, 0]).astype(np.float32),
        "b4_words": b4_words, "b4_scales": b4_scales,
        "be": (0.5 * n(H) * u[:, 0]).astype(np.float32),
        "wc": (n((H, N)) / np.sqrt(H) / u).astype(np.float32),
        "d8_words": d8_words, "d8_scales": d8_scales,
        "bo": (0.5 * n(N)).astype(np.float32),
        "wgo": np.exp(0.3 * n((128, S))).astype(np.float32),
    }

def reference(tab_words, tab_scales, offs, offs2, offs3, wa, bw, b4_words, b4_scales, be,
              wc, d8_words, d8_scales, bo, wgo):
    TW = unpack_weight(tab_words, tab_scales, "e4m3")
    v = TW[:, unstriped(offs)]
    v2 = TW[:, unstriped(offs2)]
    b4 = unpack_weight(b4_words, b4_scales, "e2m1")
    d8 = unpack_weight(d8_words, d8_scales, "e4m3")
    west = (mxq(f64(wa), 0, "e4m3").T @ v) + f64(bw)[:, None]
    east = (b4.T @ v2) + f64(be)[:, None]
    h = np.maximum(west, east)
    e = mxq(f64(wc), 0, "e4m3").T @ mxq(h, 0, "e4m3") + d8.T @ v
    y = np.tanh(e + f64(bo)[:, None])
    out = np.zeros((N, T2))
    out[:, unstriped(offs3)] = np.tile(f64(wgo), (N // 128, 1)) * y
    return out

@@ -1,0 +1,272 @@
+from contextlib import ExitStack
+
+import concourse.mybir as mybir
+
+K, H, N, T, S, T2 = 1024, 512, 512, 4096, 1024, 2048
+FLOPS = 2 * S * (2 * K * H + H * N + K * N)
+
+F32 = mybir.dt.float32
+BF16 = mybir.dt.bfloat16
+I32 = mybir.dt.int32
+U32 = mybir.dt.uint32
+U16 = mybir.dt.uint16
+U8 = mybir.dt.uint8
+FP8X4 = mybir.dt.float8_e4m3fn_x4
+FP4X4 = mybir.dt.float4_e2m1fn_x4
+ALU = mybir.AluOpType
+ACT = mybir.ActivationFunctionType
+
+P = 128
+PACK = 4
+PASSES = K // (P * PACK)
+HALF = S // 2
+CHUNK = S // 4
+PER_COL = 16
+
+
+def tile_list_cable_fault_ends_kernel(
+    tc, tab_words, tab_scales, offs, offs2, offs3, wa, bw, b4_words, b4_scales, be,
+    wc, d8_words, d8_scales, bo, wgo, out,
+):
+    nc = tc.nc
+    with ExitStack() as ctx:
+        lists = ctx.enter_context(tc.tile_pool(name="lists", bufs=1))
+        keep = ctx.enter_context(tc.tile_pool(name="keep", bufs=1))
+        psum = ctx.enter_context(tc.psum_pool(name="psum", bufs=1))
+
+        def sb(name, shape, dtype, tag=None):
+            return keep.tile(shape, dtype, name=name, tag=tag or name, align_bytes=64)
+
+        def bank(name, b):
+            return psum.tile([P, 512], F32, name=name, tag="bank%d" % b)
+
+        tab_sc = sb("tab_sc", [P, T], U8)
+        b4_sc_raw = sb("b4_sc_raw", [P, PASSES, H], U8)
+        east_sc1 = sb("east_sc1", [P, S], U8)
+        d8_sc = sb("d8_sc", [P, N], U8)
+        nc.gpsimd.memset(tab_sc[:].bitcast(I32), 0)
+        nc.gpsimd.memset(b4_sc_raw[:].bitcast(I32), 0)
+        nc.gpsimd.memset(east_sc1[:].bitcast(I32), 0)
+        nc.gpsimd.memset(d8_sc[:].bitcast(I32), 0)
+        pages = [sb("page%d" % nb, [P, T2], F32) for nb in range(N // P)]
+        for page in pages:
+            nc.gpsimd.memset(page[:], 0.0)
+
+        west_list = lists.tile([P, S // PER_COL], U16, name="west_list")
+        east_list = lists.tile([P, S // PER_COL], U16, name="east_list")
+        place_list = lists.tile([P, S // PER_COL], U16, name="place_list")
+        nc.sync.dma_start(east_list[:], offs2)
+        nc.sync.dma_start(west_list[:], offs)
+        b4_raw = sb("b4_raw", [P, PASSES, 2 * H], U8)
+        nc.sync.dma_start(b4_raw[:].bitcast(I32), b4_words.rearrange("a p c -> p a c").bitcast(I32))
+        for q in range(4):
+            nc.sync.dma_start(tab_sc[32 * q : 32 * q + 8, :].bitcast(I32), tab_scales[:, 4 * q : 4 * q + 4, :].bitcast(I32))
+        tabs = [sb("tab%d" % a, [P, T], I32) for a in range(PASSES)]
+        wa_raw = [sb("wa_raw%d" % a, [P, PACK, H], F32) for a in range(PASSES)]
+
+        def load_tab(a):
+            nc.sync.dma_start(tabs[a][:], tab_words[a].rearrange("p t i -> p (t i)").bitcast(I32))
+
+        load_tab(0)
+        for q in range(4):
+            nc.sync.dma_start(
+                b4_sc_raw[32 * q : 32 * q + 4, :, :].bitcast(I32),
+                b4_scales[:, 4 * q : 4 * q + 4, :].rearrange("a r c -> r a c").bitcast(I32),
+            )
+        for a in range(PASSES):
+            nc.sync.dma_start(wa_raw[a][:], wa[512 * a : 512 * (a + 1), :].rearrange("(p j) c -> p j c", j=PACK))
+        load_tab(1)
+
+        east_sc = sb("east_sc", [P, S], U8)
+        west_sc = sb("west_sc", [P, S], U8)
+        nc.vector.tensor_copy(east_sc[:], tab_sc[:].indirect(east_list[:]))
+        nc.vector.tensor_copy(west_sc[:], tab_sc[:].indirect(west_list[:]))
+        nc.scalar.dma_start(east_sc1[0:100, :].bitcast(I32), east_sc[4:104, :].bitcast(I32))
+
+        bw_t = sb("bw_t", [P, PACK], F32)
+        be_t = sb("be_t", [P, PACK], F32)
+        bo_t = sb("bo_t", [P, N // P], F32)
+        nc.sync.dma_start(bw_t[:], bw.rearrange("(p t) -> p t", t=PACK))
+        nc.sync.dma_start(be_t[:], be.rearrange("(p t) -> p t", t=PACK))
+        wc_raw = sb("wc_raw", [P, PACK, N], F32)
+        nc.sync.dma_start(wc_raw[:], wc.rearrange("(p j) c -> p j c", j=PACK))
+        for q in range(4):
+            nc.sync.dma_start(d8_sc[32 * q : 32 * q + 8, :].bitcast(I32), d8_scales[:, 4 * q : 4 * q + 4, :].bitcast(I32))
+        d8_w = sb("d8_w", [P, PASSES, N], I32)
+        nc.sync.dma_start(d8_w[:], d8_words.rearrange("a p c i -> p a (c i)").bitcast(I32))
+        with nc.allow_non_contiguous_dma(reason="one bias value for each partition and row block"):
+            nc.sync.dma_start(bo_t[:], bo.rearrange("(c p) -> p c", p=P))
+        nc.sync.dma_start(place_list[:], offs3)
+        wgo_t = sb("wgo_t", [P, S], F32)
+        nc.sync.dma_start(wgo_t[:], wgo)
+
+        west_w0 = sb("west_w0", [P, S], U32)
+        east_w0 = sb("east_w0", [P, S], U32)
+        nc.vector.tensor_copy(west_w0[:], tabs[0][:].bitcast(U32).indirect(west_list[:]))
+        nc.vector.tensor_copy(east_w0[:], tabs[0][:].bitcast(U32).indirect(east_list[:]))
+
+        b4_w = sb("b4_w", [P, PASSES, 2 * H], U8)
+        b4_sc = sb("b4_sc", [P, PASSES, H], U8)
+        nc.vector.tensor_copy(
+            b4_w[:].bitcast(U16).rearrange("p a (t m) -> p a t m", t=PACK),
+            b4_raw[:].bitcast(U16).rearrange("p a (m t) -> p a t m", t=PACK),
+        )
+        nc.vector.tensor_copy(
+            b4_sc[:].rearrange("p a (t m) -> p a t m", t=PACK),
+            b4_sc_raw[:].rearrange("p a (m t) -> p a t m", t=PACK),
+        )
+
+        wa_w = [sb("wa_w%d" % a, [P, H], U32) for a in range(PASSES)]
+        wa_sc = [sb("wa_sc%d" % a, [P, H], U8) for a in range(PASSES)]
+        for a in range(PASSES):
+            wa_bf = sb("wa_bf%d" % a, [P, PACK * H], BF16)
+            nc.scalar.copy(
+                wa_bf[:].rearrange("p (t m j) -> p m j t", t=PACK, j=PACK),
+                wa_raw[a][:].rearrange("p j (m t) -> p m j t", t=PACK),
+            )
+            nc.vector.quantize_mx(out=wa_w[a][:].bitcast(FP8X4), scales=wa_sc[a][:], in_=wa_bf[:])
+
+        def list_cols(lst, first, count):
+            return lst[:, first // PER_COL : (first + count) // PER_COL]
+
+        west_w1, east_w1 = {}, {}
+
+        def gather_pass1(store, name, lst, half, tag=None):
+            store[half] = sb("%s%d" % (name, half), [P, HALF], U32, tag)
+            nc.vector.tensor_copy(store[half][:], tabs[1][:].bitcast(U32).indirect(list_cols(lst, half * HALF, HALF)))
+
+        def west_operand(a, first, count):
+            words = west_w0[:, first : first + count] if a == 0 else west_w1[first // HALF][:, first % HALF : first % HALF + count]
+            return words.bitcast(FP8X4), west_sc[4 * a : P, first : first + count]
+
+        def east_operand(a, first, count):
+            words = east_w0[:, first : first + count] if a == 0 else east_w1[first // HALF][:, first % HALF : first % HALF + count]
+            plane = east_sc if a == 0 else east_sc1
+            return words.bitcast(FP8X4), plane[:, first : first + count]
+
+        def wa_operand(a, t):
+            return wa_w[a][:, P * t : P * (t + 1)].bitcast(FP8X4), wa_sc[a][:, P * t : P * (t + 1)]
+
+        def b4_operand(a, t):
+            return b4_w[:, a, 2 * P * t : 2 * P * (t + 1)].bitcast(FP4X4), b4_sc[:, a, P * t : P * (t + 1)]
+
+        def d8_operand(a, nb):
+            return d8_w[:, a, P * nb : P * (nb + 1)].bitcast(FP8X4), d8_sc[4 * a : P, P * nb : P * (nb + 1)]
+
+        def group(passes):
+            for i, (dst, (w, w_sc), (x, x_sc)) in enumerate(passes):
+                nc.tensor.matmul_mx(out=dst, lhsT=w, lhsT_scale=w_sc, rhs=x, rhs_scale=x_sc,
+                                    start=(i == 0), stop=(i == len(passes) - 1))
+
+        def first_stage(name, c, bank_ids, weight, moving):
+            sums = []
+            for u, b in enumerate(bank_ids):
+                acc = bank("%s_%d_%d" % (name, c, u), b)
+                dst = [acc[:, CHUNK * v : CHUNK * (v + 1)] for v in range(2)]
+                group([(dst[v], weight(a, 2 * u + v), moving(a, c * CHUNK, CHUNK)) for a in range(PASSES) for v in range(2)])
+                sums.extend(dst)
+            return sums
+
+        west_sb, h_planes, h_bf = {}, {}, {}
+        h_w = [sb("h_w%d" % half, [P, HALF], U32) for half in range(2)]
+        h_sc = [sb("h_sc%d" % half, [P, HALF], U8) for half in range(2)]
+
+        def west_stage(c, bank_ids):
+            sums = first_stage("west", c, bank_ids, wa_operand, west_operand)
+            west_sb[c] = sb("west_sb%d" % c, [P, PACK, CHUNK], F32)
+            for t in range(PACK):
+                nc.scalar.activation(west_sb[c][:, t, :], sums[t], ACT.Identity, bias=bw_t[:, t : t + 1])
+
+        def east_stage(c, bank_ids):
+            sums = first_stage("east", c, bank_ids, b4_operand, east_operand)
+            h_planes[c] = sb("h_planes%d" % c, [P, PACK, CHUNK], BF16)
+            for t in range(PACK):
+                nc.vector.scalar_tensor_tensor(
+                    h_planes[c][:, t, :], sums[t], be_t[:, t : t + 1], west_sb[c][:, t, :], ALU.add, ALU.max
+                )
+
+        def weave(c):
+            h_bf[c] = sb("h_bf%d" % c, [P, PACK * CHUNK], BF16)
+            nc.scalar.copy(
+                h_bf[c][:].rearrange("p (c i t) -> p c t i", i=4, t=PACK),
+                h_planes[c][:].rearrange("p t (c i) -> p c t i", i=4),
+            )
+
+        def quantise_h(c):
+            cols = slice((c % 2) * CHUNK, (c % 2 + 1) * CHUNK)
+            nc.vector.quantize_mx(out=h_w[c // 2][:, cols].bitcast(FP8X4), scales=h_sc[c // 2][:, cols], in_=h_bf[c][:])
+
+        wc_w, wc_sc = {}, {}
+
+        def quantise_wc(nb):
+            wc_bf = sb("wc_bf%d" % nb, [P, PACK * P], BF16)
+            wc_w[nb] = sb("wc_w%d" % nb, [P, P], U32)
+            wc_sc[nb] = sb("wc_sc%d" % nb, [P, P], U8)
+            nc.scalar.copy(
+                wc_bf[:].rearrange("p (c i j) -> p c j i", i=4, j=PACK),
+                wc_raw[:, :, P * nb : P * (nb + 1)].rearrange("p j (c i) -> p c j i", i=4),
+            )
+            nc.vector.quantize_mx(out=wc_w[nb][:].bitcast(FP8X4), scales=wc_sc[nb][:], in_=wc_bf[:])
+
+        y = {}
+
+        def second_stage(first, count, blocks, b, tags=None):
+            acc = bank("y_%d_%d" % (first, blocks[0]), b)
+            dst = [acc[:, count * v : count * (v + 1)] for v in range(len(blocks))]
+            cols = slice(first % HALF, first % HALF + count)
+            h_operand = (h_w[first // HALF][:, cols].bitcast(FP8X4), h_sc[first // HALF][:, cols])
+            group(
+                [(dst[v], d8_operand(a, nb), west_operand(a, first, count)) for v, nb in enumerate(blocks) for a in range(PASSES)]
+                + [(dst[v], (wc_w[nb][:].bitcast(FP8X4), wc_sc[nb][:]), h_operand) for v, nb in enumerate(blocks)]
+            )
+            for v, nb in enumerate(blocks):
+                y[first, nb] = sb("y_sb_%d_%d" % (first, nb), [P, count], F32, tags)
+                nc.scalar.activation(y[first, nb][:], dst[v], ACT.Tanh, bias=bo_t[:, nb : nb + 1])
+
+        def place(first, count, nb):
+            nc.vector.tensor_tensor(
+                pages[nb][:].indirect(list_cols(place_list, first, count)),
+                y[first, nb][:], wgo_t[:, first : first + count], ALU.mult,
+            )
+
+        def store(nb):
+            nc.sync.dma_start(out[P * nb : P * (nb + 1), :], pages[nb][:])
+
+        gather_pass1(west_w1, "west_w1_", west_list, 0)
+        gather_pass1(east_w1, "east_w1_", east_list, 0)
+        west_stage(0, (0, 1))
+        east_stage(0, (2, 3))
+        weave(0)
+        quantise_h(0)
+        quantise_wc(0)
+        quantise_wc(1)
+        west_stage(1, (4, 5))
+        second_stage(0, CHUNK, (0, 1), 0)
+        gather_pass1(west_w1, "west_w1_", west_list, 1, "west_sb0")
+        east_stage(1, (6, 7))
+        weave(1)
+        quantise_h(1)
+        gather_pass1(east_w1, "east_w1_", east_list, 1, "h_planes0")
+        west_stage(2, (1, 4))
+        west_stage(3, (5, 2))
+        east_stage(2, (3, 6))
+        weave(2)
+        east_stage(3, (7, 1))
+        second_stage(CHUNK, CHUNK, (0, 1), 5)
+        weave(3)
+        quantise_h(2)
+        quantise_h(3)
+        quantise_wc(2)
+        quantise_wc(3)
+        second_stage(0, HALF, (2,), 4)
+        second_stage(0, HALF, (3,), 2, "h_planes3")
+        place(0, CHUNK, 0)
+        place(0, CHUNK, 1)
+        place(CHUNK, CHUNK, 0)
+        place(CHUNK, CHUNK, 1)
+        place(0, HALF, 2)
+        place(0, HALF, 3)
+        for nb, b in enumerate((0, 3, 6, 7)):
+            second_stage(HALF, HALF, (nb,), b)
+            place(HALF, HALF, nb)
+            store(nb)

@@ -1,6 +1,7 @@
 from contextlib import ExitStack
 
 import concourse.mybir as mybir
+from concourse.masks import make_identity
 
 K, H, N, T, S, T2 = 1024, 512, 512, 4096, 1024, 2048
 FLOPS = 2 * S * (2 * K * H + H * N + K * N)
@@ -44,85 +45,97 @@ def tile_list_cable_fault_ends_kernel(
         b4_sc_raw = sb("b4_sc_raw", [P, PASSES, H], U8)
         east_sc1 = sb("east_sc1", [P, S], U8)
         d8_sc = sb("d8_sc", [P, N], U8)
-        nc.gpsimd.memset(tab_sc[:].bitcast(I32), 0)
-        nc.gpsimd.memset(b4_sc_raw[:].bitcast(I32), 0)
-        nc.gpsimd.memset(east_sc1[:].bitcast(I32), 0)
-        nc.gpsimd.memset(d8_sc[:].bitcast(I32), 0)
+        nc.vector.memset(tab_sc[:].bitcast(I32), 0)
+        nc.vector.memset(b4_sc_raw[:].bitcast(I32), 0)
+        nc.vector.memset(east_sc1[:].bitcast(I32), 0)
+        nc.vector.memset(d8_sc[:].bitcast(I32), 0)
         pages = [sb("page%d" % nb, [P, T2], F32) for nb in range(N // P)]
         for page in pages:
-            nc.gpsimd.memset(page[:], 0.0)
+            nc.vector.memset(page[:], 0.0)
 
         west_list = lists.tile([P, S // PER_COL], U16, name="west_list")
         east_list = lists.tile([P, S // PER_COL], U16, name="east_list")
         place_list = lists.tile([P, S // PER_COL], U16, name="place_list")
-        nc.sync.dma_start(east_list[:], offs2)
-        nc.sync.dma_start(west_list[:], offs)
-        b4_raw = sb("b4_raw", [P, PASSES, 2 * H], U8)
-        nc.sync.dma_start(b4_raw[:].bitcast(I32), b4_words.rearrange("a p c -> p a c").bitcast(I32))
-        for q in range(4):
-            nc.sync.dma_start(tab_sc[32 * q : 32 * q + 8, :].bitcast(I32), tab_scales[:, 4 * q : 4 * q + 4, :].bitcast(I32))
         tabs = [sb("tab%d" % a, [P, T], I32) for a in range(PASSES)]
         wa_raw = [sb("wa_raw%d" % a, [P, PACK, H], F32) for a in range(PASSES)]
+        b4_raw = sb("b4_raw", [P, PASSES, 2 * H], U8)
+        bias_rows = sb("bias_rows", [P, P], F32)
+        ident = sb("ident", [P, P], F32)
+        nc.gpsimd.memset(bias_rows[:], 0.0)
+        make_identity(nc, ident[:])
 
         def load_tab(a):
             nc.sync.dma_start(tabs[a][:], tab_words[a].rearrange("p t i -> p (t i)").bitcast(I32))
 
+        def load_wa(a):
+            nc.sync.dma_start(wa_raw[a][:], wa[512 * a : 512 * (a + 1), :].rearrange("(p j) c -> p j c", j=PACK))
+
+        nc.sync.dma_start(east_list[:], offs2)
+        nc.sync.dma_start(west_list[:], offs)
         load_tab(0)
+        for a in range(PASSES):
+            for q in range(4):
+                first = 32 * q + 4 * a
+                nc.sync.dma_start(tab_sc[first : first + 4, :].bitcast(I32), tab_scales[a, 4 * q : 4 * q + 4, :].bitcast(I32))
+        load_wa(0)
+        nc.sync.dma_start(b4_raw[:].bitcast(I32), b4_words.rearrange("a p c -> p a c").bitcast(I32))
         for q in range(4):
             nc.sync.dma_start(
                 b4_sc_raw[32 * q : 32 * q + 4, :, :].bitcast(I32),
                 b4_scales[:, 4 * q : 4 * q + 4, :].rearrange("a r c -> r a c").bitcast(I32),
             )
-        for a in range(PASSES):
-            nc.sync.dma_start(wa_raw[a][:], wa[512 * a : 512 * (a + 1), :].rearrange("(p j) c -> p j c", j=PACK))
+        load_wa(1)
+        for u, vec in enumerate((bw, be)):
+            nc.sync.dma_start(
+                bias_rows[PACK * u : PACK * (u + 1), :].rearrange("t (b i) -> t b i", i=8),
+                vec.rearrange("(b t i) -> t b i", t=PACK, i=8),
+            )
+        nc.sync.dma_start(bias_rows[2 * PACK : 3 * PACK, :], bo.rearrange("(c p) -> c p", p=P))
         load_tab(1)
+        bias_ps = bank("bias_ps", 7)
+        nc.tensor.transpose(bias_ps[:, 0:P], bias_rows[:], ident[:])
+        bias_cols = sb("bias_cols", [P, 3 * PACK], F32)
+        nc.scalar.copy(bias_cols[:], bias_ps[:, 0 : 3 * PACK])
+        bw_t, be_t, bo_t = (bias_cols[:, PACK * u : PACK * (u + 1)] for u in range(3))
+
+        west_w0 = sb("west_w0", [P, S], U32)
+        east_w0 = sb("east_w0", [P, S], U32)
+        nc.vector.tensor_copy(east_w0[:], tabs[0][:].bitcast(U32).indirect(east_list[:]))
 
         east_sc = sb("east_sc", [P, S], U8)
         west_sc = sb("west_sc", [P, S], U8)
         nc.vector.tensor_copy(east_sc[:], tab_sc[:].indirect(east_list[:]))
-        nc.vector.tensor_copy(west_sc[:], tab_sc[:].indirect(west_list[:]))
-        nc.scalar.dma_start(east_sc1[0:100, :].bitcast(I32), east_sc[4:104, :].bitcast(I32))
+        nc.gpsimd.dma_start(east_sc1[0:100, :].bitcast(I32), east_sc[4:104, :].bitcast(I32))
 
-        bw_t = sb("bw_t", [P, PACK], F32)
-        be_t = sb("be_t", [P, PACK], F32)
-        bo_t = sb("bo_t", [P, N // P], F32)
-        nc.sync.dma_start(bw_t[:], bw.rearrange("(p t) -> p t", t=PACK))
-        nc.sync.dma_start(be_t[:], be.rearrange("(p t) -> p t", t=PACK))
+        nc.vector.tensor_copy(west_w0[:], tabs[0][:].bitcast(U32).indirect(west_list[:]))
         wc_raw = sb("wc_raw", [P, PACK, N], F32)
-        nc.sync.dma_start(wc_raw[:], wc.rearrange("(p j) c -> p j c", j=PACK))
-        for q in range(4):
-            nc.sync.dma_start(d8_sc[32 * q : 32 * q + 8, :].bitcast(I32), d8_scales[:, 4 * q : 4 * q + 4, :].bitcast(I32))
+        for t in range(PACK):
+            nc.sync.dma_start(wc_raw[:, t, :], wc.rearrange("(b t i) c -> t b i c", t=PACK, i=8)[t])
         d8_w = sb("d8_w", [P, PASSES, N], I32)
         nc.sync.dma_start(d8_w[:], d8_words.rearrange("a p c i -> p a (c i)").bitcast(I32))
-        with nc.allow_non_contiguous_dma(reason="one bias value for each partition and row block"):
-            nc.sync.dma_start(bo_t[:], bo.rearrange("(c p) -> p c", p=P))
+        for q in range(4):
+            nc.sync.dma_start(d8_sc[32 * q : 32 * q + 8, :].bitcast(I32), d8_scales[:, 4 * q : 4 * q + 4, :].bitcast(I32))
         nc.sync.dma_start(place_list[:], offs3)
         wgo_t = sb("wgo_t", [P, S], F32)
         nc.sync.dma_start(wgo_t[:], wgo)
 
-        west_w0 = sb("west_w0", [P, S], U32)
-        east_w0 = sb("east_w0", [P, S], U32)
-        nc.vector.tensor_copy(west_w0[:], tabs[0][:].bitcast(U32).indirect(west_list[:]))
-        nc.vector.tensor_copy(east_w0[:], tabs[0][:].bitcast(U32).indirect(east_list[:]))
-
         b4_w = sb("b4_w", [P, PASSES, 2 * H], U8)
         b4_sc = sb("b4_sc", [P, PASSES, H], U8)
-        nc.vector.tensor_copy(
-            b4_w[:].bitcast(U16).rearrange("p a (t m) -> p a t m", t=PACK),
-            b4_raw[:].bitcast(U16).rearrange("p a (m t) -> p a t m", t=PACK),
-        )
-        nc.vector.tensor_copy(
-            b4_sc[:].rearrange("p a (t m) -> p a t m", t=PACK),
-            b4_sc_raw[:].rearrange("p a (m t) -> p a t m", t=PACK),
-        )
+        for dealt, raw in ((b4_w, b4_raw), (b4_sc, b4_sc_raw)):
+            nc.vector.tensor_copy(
+                dealt[:].bitcast(I32).rearrange("p a (t b w) -> p a t b w", t=PACK, b=16),
+                raw[:].bitcast(I32).rearrange("p a (b t w) -> p a t b w", t=PACK, b=16),
+            )
+
+        nc.vector.tensor_copy(west_sc[:], tab_sc[:].indirect(west_list[:]))
 
         wa_w = [sb("wa_w%d" % a, [P, H], U32) for a in range(PASSES)]
         wa_sc = [sb("wa_sc%d" % a, [P, H], U8) for a in range(PASSES)]
         for a in range(PASSES):
             wa_bf = sb("wa_bf%d" % a, [P, PACK * H], BF16)
             nc.scalar.copy(
-                wa_bf[:].rearrange("p (t m j) -> p m j t", t=PACK, j=PACK),
-                wa_raw[a][:].rearrange("p j (m t) -> p m j t", t=PACK),
+                wa_bf[:].rearrange("p (t b i j) -> p t b i j", t=PACK, i=8, j=PACK),
+                wa_raw[a][:].rearrange("p j (b t i) -> p t b i j", t=PACK, i=8),
             )
             nc.vector.quantize_mx(out=wa_w[a][:].bitcast(FP8X4), scales=wa_sc[a][:], in_=wa_bf[:])
 
@@ -177,9 +190,9 @@ def tile_list_cable_fault_ends_kernel(
             for t in range(PACK):
                 nc.scalar.activation(west_sb[c][:, t, :], sums[t], ACT.Identity, bias=bw_t[:, t : t + 1])
 
-        def east_stage(c, bank_ids):
+        def east_stage(c, bank_ids, tag=None):
             sums = first_stage("east", c, bank_ids, b4_operand, east_operand)
-            h_planes[c] = sb("h_planes%d" % c, [P, PACK, CHUNK], BF16)
+            h_planes[c] = sb("h_planes%d" % c, [P, PACK, CHUNK], BF16, tag)
             for t in range(PACK):
                 nc.vector.scalar_tensor_tensor(
                     h_planes[c][:, t, :], sums[t], be_t[:, t : t + 1], west_sb[c][:, t, :], ALU.add, ALU.max
@@ -188,8 +201,8 @@ def tile_list_cable_fault_ends_kernel(
         def weave(c):
             h_bf[c] = sb("h_bf%d" % c, [P, PACK * CHUNK], BF16)
             nc.scalar.copy(
-                h_bf[c][:].rearrange("p (c i t) -> p c t i", i=4, t=PACK),
-                h_planes[c][:].rearrange("p t (c i) -> p c t i", i=4),
+                h_bf[c][:].rearrange("p (n t) -> p n t", t=PACK),
+                h_planes[c][:].rearrange("p t n -> p n t"),
             )
 
         def quantise_h(c):
@@ -203,8 +216,8 @@ def tile_list_cable_fault_ends_kernel(
             wc_w[nb] = sb("wc_w%d" % nb, [P, P], U32)
             wc_sc[nb] = sb("wc_sc%d" % nb, [P, P], U8)
             nc.scalar.copy(
-                wc_bf[:].rearrange("p (c i j) -> p c j i", i=4, j=PACK),
-                wc_raw[:, :, P * nb : P * (nb + 1)].rearrange("p j (c i) -> p c j i", i=4),
+                wc_bf[:].rearrange("p (c j) -> p c j", j=PACK),
+                wc_raw[:, :, P * nb : P * (nb + 1)].rearrange("p j c -> p c j"),
             )
             nc.vector.quantize_mx(out=wc_w[nb][:].bitcast(FP8X4), scales=wc_sc[nb][:], in_=wc_bf[:])
 
@@ -234,6 +247,7 @@ def tile_list_cable_fault_ends_kernel(
 
         gather_pass1(west_w1, "west_w1_", west_list, 0)
         gather_pass1(east_w1, "east_w1_", east_list, 0)
+        gather_pass1(west_w1, "west_w1_", west_list, 1)
         west_stage(0, (0, 1))
         east_stage(0, (2, 3))
         weave(0)
@@ -242,22 +256,21 @@ def tile_list_cable_fault_ends_kernel(
         quantise_wc(1)
         west_stage(1, (4, 5))
         second_stage(0, CHUNK, (0, 1), 0)
-        gather_pass1(west_w1, "west_w1_", west_list, 1, "west_sb0")
-        east_stage(1, (6, 7))
+        gather_pass1(east_w1, "east_w1_", east_list, 1, "west_sb0")
+        east_stage(1, (6, 7), "h_bf0")
         weave(1)
         quantise_h(1)
-        gather_pass1(east_w1, "east_w1_", east_list, 1, "h_planes0")
         west_stage(2, (1, 4))
+        quantise_wc(2)
+        quantise_wc(3)
         west_stage(3, (5, 2))
         east_stage(2, (3, 6))
+        second_stage(CHUNK, CHUNK, (0, 1), 5)
         weave(2)
         east_stage(3, (7, 1))
-        second_stage(CHUNK, CHUNK, (0, 1), 5)
         weave(3)
         quantise_h(2)
         quantise_h(3)
-        quantise_wc(2)
-        quantise_wc(3)
         second_stage(0, HALF, (2,), 4)
         second_stage(0, HALF, (3,), 2, "h_planes3")
         place(0, CHUNK, 0)

@@ -47,10 +47,8 @@ def tile_list_cable_fault_ends_kernel(
         d8_sc = sb("d8_sc", [P, N], U8)
         nc.vector.memset(tab_sc[:].bitcast(I32), 0)
         nc.vector.memset(b4_sc_raw[:].bitcast(I32), 0)
-        nc.vector.memset(east_sc1[:].bitcast(I32), 0)
-        nc.vector.memset(d8_sc[:].bitcast(I32), 0)
         pages = [sb("page%d" % nb, [P, T2], F32) for nb in range(N // P)]
-        for page in pages:
+        for page in pages[0:2]:
             nc.vector.memset(page[:], 0.0)
 
         west_list = lists.tile([P, S // PER_COL], U16, name="west_list")
@@ -63,6 +61,10 @@ def tile_list_cable_fault_ends_kernel(
         ident = sb("ident", [P, P], F32)
         nc.gpsimd.memset(bias_rows[:], 0.0)
         make_identity(nc, ident[:])
+        nc.gpsimd.memset(east_sc1[:].bitcast(I32), 0)
+        nc.gpsimd.memset(d8_sc[:].bitcast(I32), 0)
+        for page in pages[2:4]:
+            nc.gpsimd.memset(page[:], 0.0)
 
         def load_tab(a):
             nc.sync.dma_start(tabs[a][:], tab_words[a].rearrange("p t i -> p (t i)").bitcast(I32))
@@ -77,13 +79,13 @@ def tile_list_cable_fault_ends_kernel(
             for q in range(4):
                 first = 32 * q + 4 * a
                 nc.sync.dma_start(tab_sc[first : first + 4, :].bitcast(I32), tab_scales[a, 4 * q : 4 * q + 4, :].bitcast(I32))
-        load_wa(0)
         nc.sync.dma_start(b4_raw[:].bitcast(I32), b4_words.rearrange("a p c -> p a c").bitcast(I32))
         for q in range(4):
             nc.sync.dma_start(
                 b4_sc_raw[32 * q : 32 * q + 4, :, :].bitcast(I32),
                 b4_scales[:, 4 * q : 4 * q + 4, :].rearrange("a r c -> r a c").bitcast(I32),
             )
+        load_wa(0)
         load_wa(1)
         for u, vec in enumerate((bw, be)):
             nc.sync.dma_start(
@@ -103,7 +105,6 @@ def tile_list_cable_fault_ends_kernel(
         nc.vector.tensor_copy(east_w0[:], tabs[0][:].bitcast(U32).indirect(east_list[:]))
 
         east_sc = sb("east_sc", [P, S], U8)
-        west_sc = sb("west_sc", [P, S], U8)
         nc.vector.tensor_copy(east_sc[:], tab_sc[:].indirect(east_list[:]))
         nc.gpsimd.dma_start(east_sc1[0:100, :].bitcast(I32), east_sc[4:104, :].bitcast(I32))
 
@@ -127,6 +128,7 @@ def tile_list_cable_fault_ends_kernel(
                 raw[:].bitcast(I32).rearrange("p a (b t w) -> p a t b w", t=PACK, b=16),
             )
 
+        west_sc = sb("west_sc", [P, S], U8, "b4_sc_raw")
         nc.vector.tensor_copy(west_sc[:], tab_sc[:].indirect(west_list[:]))
 
         wa_w = [sb("wa_w%d" % a, [P, H], U32) for a in range(PASSES)]
@@ -171,12 +173,13 @@ def tile_list_cable_fault_ends_kernel(
                 nc.tensor.matmul_mx(out=dst, lhsT=w, lhsT_scale=w_sc, rhs=x, rhs_scale=x_sc,
                                     start=(i == 0), stop=(i == len(passes) - 1))
 
-        def first_stage(name, c, bank_ids, weight, moving):
+        def first_stage(name, first, count, bank_ids, weight, moving):
+            per_bank = PACK // len(bank_ids)
             sums = []
             for u, b in enumerate(bank_ids):
-                acc = bank("%s_%d_%d" % (name, c, u), b)
-                dst = [acc[:, CHUNK * v : CHUNK * (v + 1)] for v in range(2)]
-                group([(dst[v], weight(a, 2 * u + v), moving(a, c * CHUNK, CHUNK)) for a in range(PASSES) for v in range(2)])
+                acc = bank("%s_%d_%d" % (name, first, u), b)
+                dst = [acc[:, count * v : count * (v + 1)] for v in range(per_bank)]
+                group([(dst[v], weight(a, per_bank * u + v), moving(a, first, count)) for a in range(PASSES) for v in range(per_bank)])
                 sums.extend(dst)
             return sums
 
@@ -184,42 +187,46 @@ def tile_list_cable_fault_ends_kernel(
         h_w = [sb("h_w%d" % half, [P, HALF], U32) for half in range(2)]
         h_sc = [sb("h_sc%d" % half, [P, HALF], U8) for half in range(2)]
 
-        def west_stage(c, bank_ids):
-            sums = first_stage("west", c, bank_ids, wa_operand, west_operand)
-            west_sb[c] = sb("west_sb%d" % c, [P, PACK, CHUNK], F32)
+        def west_stage(first, count, bank_ids):
+            sums = first_stage("west", first, count, bank_ids, wa_operand, west_operand)
+            west_sb[first] = sb("west_sb%d" % first, [P, PACK, count], F32)
             for t in range(PACK):
-                nc.scalar.activation(west_sb[c][:, t, :], sums[t], ACT.Identity, bias=bw_t[:, t : t + 1])
+                nc.scalar.activation(west_sb[first][:, t, :], sums[t], ACT.Identity, bias=bw_t[:, t : t + 1])
 
-        def east_stage(c, bank_ids, tag=None):
-            sums = first_stage("east", c, bank_ids, b4_operand, east_operand)
-            h_planes[c] = sb("h_planes%d" % c, [P, PACK, CHUNK], BF16, tag)
+        def east_stage(first, count, bank_ids, tag=None):
+            sums = first_stage("east", first, count, bank_ids, b4_operand, east_operand)
+            h_planes[first] = sb("h_planes%d" % first, [P, PACK, count], BF16, tag)
             for t in range(PACK):
                 nc.vector.scalar_tensor_tensor(
-                    h_planes[c][:, t, :], sums[t], be_t[:, t : t + 1], west_sb[c][:, t, :], ALU.add, ALU.max
+                    h_planes[first][:, t, :], sums[t], be_t[:, t : t + 1], west_sb[first][:, t, :], ALU.add, ALU.max
                 )
 
-        def weave(c):
-            h_bf[c] = sb("h_bf%d" % c, [P, PACK * CHUNK], BF16)
+        def weave(first, count):
+            h_bf[first] = sb("h_bf%d" % first, [P, PACK * count], BF16)
             nc.scalar.copy(
-                h_bf[c][:].rearrange("p (n t) -> p n t", t=PACK),
-                h_planes[c][:].rearrange("p t n -> p n t"),
+                h_bf[first][:].rearrange("p (n t) -> p n t", t=PACK),
+                h_planes[first][:].rearrange("p t n -> p n t"),
             )
 
-        def quantise_h(c):
-            cols = slice((c % 2) * CHUNK, (c % 2 + 1) * CHUNK)
-            nc.vector.quantize_mx(out=h_w[c // 2][:, cols].bitcast(FP8X4), scales=h_sc[c // 2][:, cols], in_=h_bf[c][:])
+        def quantise_h(first, count):
+            cols = slice(first % HALF, first % HALF + count)
+            nc.vector.quantize_mx(out=h_w[first // HALF][:, cols].bitcast(FP8X4), scales=h_sc[first // HALF][:, cols], in_=h_bf[first][:])
 
         wc_w, wc_sc = {}, {}
 
-        def quantise_wc(nb):
-            wc_bf = sb("wc_bf%d" % nb, [P, PACK * P], BF16)
-            wc_w[nb] = sb("wc_w%d" % nb, [P, P], U32)
-            wc_sc[nb] = sb("wc_sc%d" % nb, [P, P], U8)
+        def quantise_wc(u):
+            wc_bf = sb("wc_bf%d" % u, [P, PACK * 2 * P], BF16)
+            wc_w[u] = sb("wc_w%d" % u, [P, 2 * P], U32)
+            wc_sc[u] = sb("wc_sc%d" % u, [P, 2 * P], U8)
             nc.scalar.copy(
                 wc_bf[:].rearrange("p (c j) -> p c j", j=PACK),
-                wc_raw[:, :, P * nb : P * (nb + 1)].rearrange("p j c -> p c j"),
+                wc_raw[:, :, 2 * P * u : 2 * P * (u + 1)].rearrange("p j c -> p c j"),
             )
-            nc.vector.quantize_mx(out=wc_w[nb][:].bitcast(FP8X4), scales=wc_sc[nb][:], in_=wc_bf[:])
+            nc.vector.quantize_mx(out=wc_w[u][:].bitcast(FP8X4), scales=wc_sc[u][:], in_=wc_bf[:])
+
+        def wc_operand(nb):
+            cols = slice(P * (nb % 2), P * (nb % 2 + 1))
+            return wc_w[nb // 2][:, cols].bitcast(FP8X4), wc_sc[nb // 2][:, cols]
 
         y = {}
 
@@ -230,7 +237,7 @@ def tile_list_cable_fault_ends_kernel(
             h_operand = (h_w[first // HALF][:, cols].bitcast(FP8X4), h_sc[first // HALF][:, cols])
             group(
                 [(dst[v], d8_operand(a, nb), west_operand(a, first, count)) for v, nb in enumerate(blocks) for a in range(PASSES)]
-                + [(dst[v], (wc_w[nb][:].bitcast(FP8X4), wc_sc[nb][:]), h_operand) for v, nb in enumerate(blocks)]
+                + [(dst[v], wc_operand(nb), h_operand) for v, nb in enumerate(blocks)]
             )
             for v, nb in enumerate(blocks):
                 y[first, nb] = sb("y_sb_%d_%d" % (first, nb), [P, count], F32, tags)
@@ -248,38 +255,32 @@ def tile_list_cable_fault_ends_kernel(
         gather_pass1(west_w1, "west_w1_", west_list, 0)
         gather_pass1(east_w1, "east_w1_", east_list, 0)
         gather_pass1(west_w1, "west_w1_", west_list, 1)
-        west_stage(0, (0, 1))
-        east_stage(0, (2, 3))
-        weave(0)
-        quantise_h(0)
+        west_stage(0, CHUNK, (0, 1))
+        east_stage(0, CHUNK, (2, 3))
+        weave(0, CHUNK)
+        quantise_h(0, CHUNK)
         quantise_wc(0)
-        quantise_wc(1)
-        west_stage(1, (4, 5))
+        west_stage(CHUNK, CHUNK, (4, 5))
         second_stage(0, CHUNK, (0, 1), 0)
         gather_pass1(east_w1, "east_w1_", east_list, 1, "west_sb0")
-        east_stage(1, (6, 7), "h_bf0")
-        weave(1)
-        quantise_h(1)
-        west_stage(2, (1, 4))
-        quantise_wc(2)
-        quantise_wc(3)
-        west_stage(3, (5, 2))
-        east_stage(2, (3, 6))
-        second_stage(CHUNK, CHUNK, (0, 1), 5)
-        weave(2)
-        east_stage(3, (7, 1))
-        weave(3)
-        quantise_h(2)
-        quantise_h(3)
+        east_stage(CHUNK, CHUNK, (6, 7), "h_bf0")
+        weave(CHUNK, CHUNK)
+        quantise_h(CHUNK, CHUNK)
+        west_stage(HALF, HALF, (1, 4, 5, 2))
+        quantise_wc(1)
+        east_stage(HALF, HALF, (3, 6, 7, 0))
+        second_stage(CHUNK, CHUNK, (0, 1), 1)
+        weave(HALF, HALF)
+        quantise_h(HALF, HALF)
         second_stage(0, HALF, (2,), 4)
-        second_stage(0, HALF, (3,), 2, "h_planes3")
+        second_stage(0, HALF, (3,), 5, "h_planes%d" % HALF)
         place(0, CHUNK, 0)
         place(0, CHUNK, 1)
         place(CHUNK, CHUNK, 0)
         place(CHUNK, CHUNK, 1)
         place(0, HALF, 2)
         place(0, HALF, 3)
-        for nb, b in enumerate((0, 3, 6, 7)):
+        for nb, b in enumerate((2, 3, 6, 7)):
             second_stage(HALF, HALF, (nb,), b)
             place(HALF, HALF, nb)
             store(nb)

@@ -43,13 +43,27 @@ def tile_list_cable_fault_ends_kernel(
 
         tab_sc = sb("tab_sc", [P, T], U8)
         b4_sc_raw = sb("b4_sc_raw", [P, PASSES, H], U8)
-        east_sc1 = sb("east_sc1", [P, S], U8)
+        picked_sc1 = sb("picked_sc1", [P, 2 * S], U8)
         d8_sc = sb("d8_sc", [P, N], U8)
+        bias_rows = sb("bias_rows", [P, P], F32)
+        ident = sb("ident", [P, P], F32)
         nc.vector.memset(tab_sc[:].bitcast(I32), 0)
         nc.vector.memset(b4_sc_raw[:].bitcast(I32), 0)
+        nc.vector.memset(picked_sc1[:].bitcast(I32), 0)
         pages = [sb("page%d" % nb, [P, T2], F32) for nb in range(N // P)]
-        for page in pages[0:2]:
+        for page in pages:
             nc.vector.memset(page[:], 0.0)
+        nc.gpsimd.memset(bias_rows[:], 0.0)
+        nc.gpsimd.memset(d8_sc[:].bitcast(I32), 0)
+        for u, vec in enumerate((bw, be)):
+            nc.gpsimd.dma_start(
+                bias_rows[PACK * u : PACK * (u + 1), :].rearrange("t (b i) -> t b i", i=8),
+                vec.rearrange("(b t i) -> t b i", t=PACK, i=8),
+            )
+        nc.gpsimd.dma_start(bias_rows[2 * PACK : 3 * PACK, :], bo.rearrange("(c p) -> c p", p=P))
+        make_identity(nc, ident[:])
+        for q in range(4):
+            nc.gpsimd.dma_start(d8_sc[32 * q : 32 * q + 8, :].bitcast(I32), d8_scales[:, 4 * q : 4 * q + 4, :].bitcast(I32))
 
         west_list = lists.tile([P, S // PER_COL], U16, name="west_list")
         east_list = lists.tile([P, S // PER_COL], U16, name="east_list")
@@ -57,14 +71,6 @@ def tile_list_cable_fault_ends_kernel(
         tabs = [sb("tab%d" % a, [P, T], I32) for a in range(PASSES)]
         wa_raw = [sb("wa_raw%d" % a, [P, PACK, H], F32) for a in range(PASSES)]
         b4_raw = sb("b4_raw", [P, PASSES, 2 * H], U8)
-        bias_rows = sb("bias_rows", [P, P], F32)
-        ident = sb("ident", [P, P], F32)
-        nc.gpsimd.memset(bias_rows[:], 0.0)
-        make_identity(nc, ident[:])
-        nc.gpsimd.memset(east_sc1[:].bitcast(I32), 0)
-        nc.gpsimd.memset(d8_sc[:].bitcast(I32), 0)
-        for page in pages[2:4]:
-            nc.gpsimd.memset(page[:], 0.0)
 
         def load_tab(a):
             nc.sync.dma_start(tabs[a][:], tab_words[a].rearrange("p t i -> p (t i)").bitcast(I32))
@@ -72,28 +78,24 @@ def tile_list_cable_fault_ends_kernel(
         def load_wa(a):
             nc.sync.dma_start(wa_raw[a][:], wa[512 * a : 512 * (a + 1), :].rearrange("(p j) c -> p j c", j=PACK))
 
-        nc.sync.dma_start(east_list[:], offs2)
         nc.sync.dma_start(west_list[:], offs)
+        nc.sync.dma_start(east_list[:], offs2)
         load_tab(0)
-        for a in range(PASSES):
-            for q in range(4):
-                first = 32 * q + 4 * a
-                nc.sync.dma_start(tab_sc[first : first + 4, :].bitcast(I32), tab_scales[a, 4 * q : 4 * q + 4, :].bitcast(I32))
+        for r in range(4):
+            nc.sync.dma_start(
+                tab_sc[r : P : 16, :].bitcast(I32),
+                tab_scales.rearrange("a (q r) t -> r q a t", r=4)[r].bitcast(I32),
+            )
+        load_wa(0)
+        load_wa(1)
         nc.sync.dma_start(b4_raw[:].bitcast(I32), b4_words.rearrange("a p c -> p a c").bitcast(I32))
         for q in range(4):
             nc.sync.dma_start(
                 b4_sc_raw[32 * q : 32 * q + 4, :, :].bitcast(I32),
                 b4_scales[:, 4 * q : 4 * q + 4, :].rearrange("a r c -> r a c").bitcast(I32),
             )
-        load_wa(0)
-        load_wa(1)
-        for u, vec in enumerate((bw, be)):
-            nc.sync.dma_start(
-                bias_rows[PACK * u : PACK * (u + 1), :].rearrange("t (b i) -> t b i", i=8),
-                vec.rearrange("(b t i) -> t b i", t=PACK, i=8),
-            )
-        nc.sync.dma_start(bias_rows[2 * PACK : 3 * PACK, :], bo.rearrange("(c p) -> c p", p=P))
         load_tab(1)
+        nc.sync.dma_start(place_list[:], offs3)
         bias_ps = bank("bias_ps", 7)
         nc.tensor.transpose(bias_ps[:, 0:P], bias_rows[:], ident[:])
         bias_cols = sb("bias_cols", [P, 3 * PACK], F32)
@@ -102,23 +104,21 @@ def tile_list_cable_fault_ends_kernel(
 
         west_w0 = sb("west_w0", [P, S], U32)
         east_w0 = sb("east_w0", [P, S], U32)
+        picked_sc = sb("picked_sc", [P, 2 * S], U8)
+        nc.vector.tensor_copy(west_w0[:], tabs[0][:].bitcast(U32).indirect(west_list[:]))
+        nc.vector.tensor_copy(picked_sc[:, 0:S], tab_sc[:].indirect(west_list[:]))
+        nc.vector.tensor_copy(picked_sc[:, S : 2 * S], tab_sc[:].indirect(east_list[:]))
+        nc.sync.dma_start(picked_sc1[0:100, :].bitcast(I32), picked_sc[16:116, :].bitcast(I32))
         nc.vector.tensor_copy(east_w0[:], tabs[0][:].bitcast(U32).indirect(east_list[:]))
 
-        east_sc = sb("east_sc", [P, S], U8)
-        nc.vector.tensor_copy(east_sc[:], tab_sc[:].indirect(east_list[:]))
-        nc.gpsimd.dma_start(east_sc1[0:100, :].bitcast(I32), east_sc[4:104, :].bitcast(I32))
-
-        nc.vector.tensor_copy(west_w0[:], tabs[0][:].bitcast(U32).indirect(west_list[:]))
-        wc_raw = sb("wc_raw", [P, PACK, N], F32)
+        late = sb("late", [P, PACK * N + S], F32, "tab_sc")
+        wc_raw = late[:, 0 : PACK * N].rearrange("p (j c) -> p j c", j=PACK)
+        wgo_t = late[:, PACK * N : PACK * N + S]
         for t in range(PACK):
             nc.sync.dma_start(wc_raw[:, t, :], wc.rearrange("(b t i) c -> t b i c", t=PACK, i=8)[t])
-        d8_w = sb("d8_w", [P, PASSES, N], I32)
+        d8_w = sb("d8_w", [P, PASSES, N], I32, "tab0")
         nc.sync.dma_start(d8_w[:], d8_words.rearrange("a p c i -> p a (c i)").bitcast(I32))
-        for q in range(4):
-            nc.sync.dma_start(d8_sc[32 * q : 32 * q + 8, :].bitcast(I32), d8_scales[:, 4 * q : 4 * q + 4, :].bitcast(I32))
-        nc.sync.dma_start(place_list[:], offs3)
-        wgo_t = sb("wgo_t", [P, S], F32)
-        nc.sync.dma_start(wgo_t[:], wgo)
+        nc.sync.dma_start(wgo_t, wgo)
 
         b4_w = sb("b4_w", [P, PASSES, 2 * H], U8)
         b4_sc = sb("b4_sc", [P, PASSES, H], U8)
@@ -127,9 +127,6 @@ def tile_list_cable_fault_ends_kernel(
                 dealt[:].bitcast(I32).rearrange("p a (t b w) -> p a t b w", t=PACK, b=16),
                 raw[:].bitcast(I32).rearrange("p a (b t w) -> p a t b w", t=PACK, b=16),
             )
-
-        west_sc = sb("west_sc", [P, S], U8, "b4_sc_raw")
-        nc.vector.tensor_copy(west_sc[:], tab_sc[:].indirect(west_list[:]))
 
         wa_w = [sb("wa_w%d" % a, [P, H], U32) for a in range(PASSES)]
         wa_sc = [sb("wa_sc%d" % a, [P, H], U8) for a in range(PASSES)]
@@ -152,12 +149,11 @@ def tile_list_cable_fault_ends_kernel(
 
         def west_operand(a, first, count):
             words = west_w0[:, first : first + count] if a == 0 else west_w1[first // HALF][:, first % HALF : first % HALF + count]
-            return words.bitcast(FP8X4), west_sc[4 * a : P, first : first + count]
+            return words.bitcast(FP8X4), (picked_sc, picked_sc1)[a][:, first : first + count]
 
         def east_operand(a, first, count):
             words = east_w0[:, first : first + count] if a == 0 else east_w1[first // HALF][:, first % HALF : first % HALF + count]
-            plane = east_sc if a == 0 else east_sc1
-            return words.bitcast(FP8X4), plane[:, first : first + count]
+            return words.bitcast(FP8X4), (picked_sc, picked_sc1)[a][:, S + first : S + first + count]
 
         def wa_operand(a, t):
             return wa_w[a][:, P * t : P * (t + 1)].bitcast(FP8X4), wa_sc[a][:, P * t : P * (t + 1)]

@@ -44,7 +44,6 @@ def tile_list_cable_fault_ends_kernel(
         tab_sc = sb("tab_sc", [P, T], U8)
         b4_sc_raw = sb("b4_sc_raw", [P, PASSES, H], U8)
         picked_sc1 = sb("picked_sc1", [P, 2 * S], U8)
-        d8_sc = sb("d8_sc", [P, N], U8)
         bias_rows = sb("bias_rows", [P, P], F32)
         ident = sb("ident", [P, P], F32)
         nc.vector.memset(tab_sc[:].bitcast(I32), 0)
@@ -54,16 +53,7 @@ def tile_list_cable_fault_ends_kernel(
         for page in pages:
             nc.vector.memset(page[:], 0.0)
         nc.gpsimd.memset(bias_rows[:], 0.0)
-        nc.gpsimd.memset(d8_sc[:].bitcast(I32), 0)
-        for u, vec in enumerate((bw, be)):
-            nc.gpsimd.dma_start(
-                bias_rows[PACK * u : PACK * (u + 1), :].rearrange("t (b i) -> t b i", i=8),
-                vec.rearrange("(b t i) -> t b i", t=PACK, i=8),
-            )
-        nc.gpsimd.dma_start(bias_rows[2 * PACK : 3 * PACK, :], bo.rearrange("(c p) -> c p", p=P))
         make_identity(nc, ident[:])
-        for q in range(4):
-            nc.gpsimd.dma_start(d8_sc[32 * q : 32 * q + 8, :].bitcast(I32), d8_scales[:, 4 * q : 4 * q + 4, :].bitcast(I32))
 
         west_list = lists.tile([P, S // PER_COL], U16, name="west_list")
         east_list = lists.tile([P, S // PER_COL], U16, name="east_list")
@@ -80,6 +70,12 @@ def tile_list_cable_fault_ends_kernel(
 
         nc.sync.dma_start(west_list[:], offs)
         nc.sync.dma_start(east_list[:], offs2)
+        for u, vec in enumerate((bw, be)):
+            nc.sync.dma_start(
+                bias_rows[PACK * u : PACK * (u + 1), :].rearrange("t (b i) -> t b i", i=8),
+                vec.rearrange("(b t i) -> t b i", t=PACK, i=8),
+            )
+        nc.sync.dma_start(bias_rows[2 * PACK : 3 * PACK, :], bo.rearrange("(c p) -> c p", p=P))
         load_tab(0)
         for r in range(4):
             nc.sync.dma_start(
@@ -111,14 +107,11 @@ def tile_list_cable_fault_ends_kernel(
         nc.sync.dma_start(picked_sc1[0:100, :].bitcast(I32), picked_sc[16:116, :].bitcast(I32))
         nc.vector.tensor_copy(east_w0[:], tabs[0][:].bitcast(U32).indirect(east_list[:]))
 
-        late = sb("late", [P, PACK * N + S], F32, "tab_sc")
-        wc_raw = late[:, 0 : PACK * N].rearrange("p (j c) -> p j c", j=PACK)
-        wgo_t = late[:, PACK * N : PACK * N + S]
+        wc_raw = sb("wc_raw", [P, PACK, N], F32, "tab_sc")
         for t in range(PACK):
             nc.sync.dma_start(wc_raw[:, t, :], wc.rearrange("(b t i) c -> t b i c", t=PACK, i=8)[t])
         d8_w = sb("d8_w", [P, PASSES, N], I32, "tab0")
         nc.sync.dma_start(d8_w[:], d8_words.rearrange("a p c i -> p a (c i)").bitcast(I32))
-        nc.sync.dma_start(wgo_t, wgo)
 
         b4_w = sb("b4_w", [P, PASSES, 2 * H], U8)
         b4_sc = sb("b4_sc", [P, PASSES, H], U8)
@@ -127,6 +120,11 @@ def tile_list_cable_fault_ends_kernel(
                 dealt[:].bitcast(I32).rearrange("p a (t b w) -> p a t b w", t=PACK, b=16),
                 raw[:].bitcast(I32).rearrange("p a (b t w) -> p a t b w", t=PACK, b=16),
             )
+
+        d8_sc = sb("d8_sc", [P, N], U8, "b4_sc_raw")
+        nc.vector.memset(d8_sc[:].bitcast(I32), 0)
+        for q in range(4):
+            nc.sync.dma_start(d8_sc[32 * q : 32 * q + 8, :].bitcast(I32), d8_scales[:, 4 * q : 4 * q + 4, :].bitcast(I32))
 
         wa_w = [sb("wa_w%d" % a, [P, H], U32) for a in range(PASSES)]
         wa_sc = [sb("wa_sc%d" % a, [P, H], U8) for a in range(PASSES)]
@@ -137,6 +135,9 @@ def tile_list_cable_fault_ends_kernel(
                 wa_raw[a][:].rearrange("p j (b t i) -> p t b i j", t=PACK, i=8),
             )
             nc.vector.quantize_mx(out=wa_w[a][:].bitcast(FP8X4), scales=wa_sc[a][:], in_=wa_bf[:])
+
+        wgo_t = sb("wgo_t", [P, S], F32, "wa_bf0")
+        nc.sync.dma_start(wgo_t[:], wgo)
 
         def list_cols(lst, first, count):
             return lst[:, first // PER_COL : (first + count) // PER_COL]

from contextlib import ExitStack

import concourse.mybir as mybir
from concourse.masks import make_identity

K, H, N, T, S, T2 = 1024, 512, 512, 4096, 1024, 2048
FLOPS = 2 * S * (2 * K * H + H * N + K * N)

F32 = mybir.dt.float32
BF16 = mybir.dt.bfloat16
I32 = mybir.dt.int32
U32 = mybir.dt.uint32
U16 = mybir.dt.uint16
U8 = mybir.dt.uint8
FP8X4 = mybir.dt.float8_e4m3fn_x4
FP4X4 = mybir.dt.float4_e2m1fn_x4
ALU = mybir.AluOpType
ACT = mybir.ActivationFunctionType

P = 128
PACK = 4
PASSES = K // (P * PACK)
HALF = S // 2
CHUNK = S // 4
PER_COL = 16


def tile_list_cable_fault_ends_kernel(
    tc, tab_words, tab_scales, offs, offs2, offs3, wa, bw, b4_words, b4_scales, be,
    wc, d8_words, d8_scales, bo, wgo, out,
):
    nc = tc.nc
    with ExitStack() as ctx:
        lists = ctx.enter_context(tc.tile_pool(name="lists", bufs=1))
        keep = ctx.enter_context(tc.tile_pool(name="keep", bufs=1))
        psum = ctx.enter_context(tc.psum_pool(name="psum", bufs=1))

        def sb(name, shape, dtype, tag=None):
            return keep.tile(shape, dtype, name=name, tag=tag or name, align_bytes=64)

        def bank(name, b):
            return psum.tile([P, 512], F32, name=name, tag="bank%d" % b)

        tab_sc = sb("tab_sc", [P, T], U8)
        b4_sc_raw = sb("b4_sc_raw", [P, PASSES, H], U8)
        picked_sc1 = sb("picked_sc1", [P, 2 * S], U8)
        bias_rows = sb("bias_rows", [P, P], F32)
        ident = sb("ident", [P, P], F32)
        nc.vector.memset(tab_sc[:].bitcast(I32), 0)
        nc.vector.memset(b4_sc_raw[:].bitcast(I32), 0)
        nc.vector.memset(picked_sc1[:].bitcast(I32), 0)
        pages = [sb("page%d" % nb, [P, T2], F32) for nb in range(N // P)]
        for page in pages:
            nc.vector.memset(page[:], 0.0)
        nc.gpsimd.memset(bias_rows[:], 0.0)
        make_identity(nc, ident[:])

        west_list = lists.tile([P, S // PER_COL], U16, name="west_list")
        east_list = lists.tile([P, S // PER_COL], U16, name="east_list")
        place_list = lists.tile([P, S // PER_COL], U16, name="place_list")
        tabs = [sb("tab%d" % a, [P, T], I32) for a in range(PASSES)]
        wa_raw = [sb("wa_raw%d" % a, [P, PACK, H], F32) for a in range(PASSES)]
        b4_raw = sb("b4_raw", [P, PASSES, 2 * H], U8)

        def load_tab(a):
            nc.sync.dma_start(tabs[a][:], tab_words[a].rearrange("p t i -> p (t i)").bitcast(I32))

        def load_wa(a):
            nc.sync.dma_start(wa_raw[a][:], wa[512 * a : 512 * (a + 1), :].rearrange("(p j) c -> p j c", j=PACK))

        nc.sync.dma_start(west_list[:], offs)
        nc.sync.dma_start(east_list[:], offs2)
        for u, vec in enumerate((bw, be)):
            nc.sync.dma_start(
                bias_rows[PACK * u : PACK * (u + 1), :].rearrange("t (b i) -> t b i", i=8),
                vec.rearrange("(b t i) -> t b i", t=PACK, i=8),
            )
        nc.sync.dma_start(bias_rows[2 * PACK : 3 * PACK, :], bo.rearrange("(c p) -> c p", p=P))
        load_tab(0)
        for r in range(4):
            nc.sync.dma_start(
                tab_sc[r : P : 16, :].bitcast(I32),
                tab_scales.rearrange("a (q r) t -> r q a t", r=4)[r].bitcast(I32),
            )
        load_wa(0)
        load_wa(1)
        nc.sync.dma_start(b4_raw[:].bitcast(I32), b4_words.rearrange("a p c -> p a c").bitcast(I32))
        for q in range(4):
            nc.sync.dma_start(
                b4_sc_raw[32 * q : 32 * q + 4, :, :].bitcast(I32),
                b4_scales[:, 4 * q : 4 * q + 4, :].rearrange("a r c -> r a c").bitcast(I32),
            )
        load_tab(1)
        nc.sync.dma_start(place_list[:], offs3)
        bias_ps = bank("bias_ps", 7)
        nc.tensor.transpose(bias_ps[:, 0:P], bias_rows[:], ident[:])
        bias_cols = sb("bias_cols", [P, 3 * PACK], F32)
        nc.scalar.copy(bias_cols[:], bias_ps[:, 0 : 3 * PACK])
        bw_t, be_t, bo_t = (bias_cols[:, PACK * u : PACK * (u + 1)] for u in range(3))

        west_w0 = sb("west_w0", [P, S], U32)
        east_w0 = sb("east_w0", [P, S], U32)
        picked_sc = sb("picked_sc", [P, 2 * S], U8)
        nc.vector.tensor_copy(west_w0[:], tabs[0][:].bitcast(U32).indirect(west_list[:]))
        nc.vector.tensor_copy(picked_sc[:, 0:S], tab_sc[:].indirect(west_list[:]))
        nc.vector.tensor_copy(picked_sc[:, S : 2 * S], tab_sc[:].indirect(east_list[:]))
        nc.sync.dma_start(picked_sc1[0:100, :].bitcast(I32), picked_sc[16:116, :].bitcast(I32))
        nc.vector.tensor_copy(east_w0[:], tabs[0][:].bitcast(U32).indirect(east_list[:]))

        wc_raw = sb("wc_raw", [P, PACK, N], F32, "tab_sc")
        for t in range(PACK):
            nc.sync.dma_start(wc_raw[:, t, :], wc.rearrange("(b t i) c -> t b i c", t=PACK, i=8)[t])
        d8_w = sb("d8_w", [P, PASSES, N], I32, "tab0")
        nc.sync.dma_start(d8_w[:], d8_words.rearrange("a p c i -> p a (c i)").bitcast(I32))

        b4_w = sb("b4_w", [P, PASSES, 2 * H], U8)
        b4_sc = sb("b4_sc", [P, PASSES, H], U8)
        for dealt, raw in ((b4_w, b4_raw), (b4_sc, b4_sc_raw)):
            nc.vector.tensor_copy(
                dealt[:].bitcast(I32).rearrange("p a (t b w) -> p a t b w", t=PACK, b=16),
                raw[:].bitcast(I32).rearrange("p a (b t w) -> p a t b w", t=PACK, b=16),
            )

        d8_sc = sb("d8_sc", [P, N], U8, "b4_sc_raw")
        nc.vector.memset(d8_sc[:].bitcast(I32), 0)
        for q in range(4):
            nc.sync.dma_start(d8_sc[32 * q : 32 * q + 8, :].bitcast(I32), d8_scales[:, 4 * q : 4 * q + 4, :].bitcast(I32))

        wa_w = [sb("wa_w%d" % a, [P, H], U32) for a in range(PASSES)]
        wa_sc = [sb("wa_sc%d" % a, [P, H], U8) for a in range(PASSES)]
        for a in range(PASSES):
            wa_bf = sb("wa_bf%d" % a, [P, PACK * H], BF16)
            nc.scalar.copy(
                wa_bf[:].rearrange("p (t b i j) -> p t b i j", t=PACK, i=8, j=PACK),
                wa_raw[a][:].rearrange("p j (b t i) -> p t b i j", t=PACK, i=8),
            )
            nc.vector.quantize_mx(out=wa_w[a][:].bitcast(FP8X4), scales=wa_sc[a][:], in_=wa_bf[:])

        wgo_t = sb("wgo_t", [P, S], F32, "wa_bf0")
        nc.sync.dma_start(wgo_t[:], wgo)

        def list_cols(lst, first, count):
            return lst[:, first // PER_COL : (first + count) // PER_COL]

        west_w1, east_w1 = {}, {}

        def gather_pass1(store, name, lst, half, tag=None):
            store[half] = sb("%s%d" % (name, half), [P, HALF], U32, tag)
            nc.vector.tensor_copy(store[half][:], tabs[1][:].bitcast(U32).indirect(list_cols(lst, half * HALF, HALF)))

        def west_operand(a, first, count):
            words = west_w0[:, first : first + count] if a == 0 else west_w1[first // HALF][:, first % HALF : first % HALF + count]
            return words.bitcast(FP8X4), (picked_sc, picked_sc1)[a][:, first : first + count]

        def east_operand(a, first, count):
            words = east_w0[:, first : first + count] if a == 0 else east_w1[first // HALF][:, first % HALF : first % HALF + count]
            return words.bitcast(FP8X4), (picked_sc, picked_sc1)[a][:, S + first : S + first + count]

        def wa_operand(a, t):
            return wa_w[a][:, P * t : P * (t + 1)].bitcast(FP8X4), wa_sc[a][:, P * t : P * (t + 1)]

        def b4_operand(a, t):
            return b4_w[:, a, 2 * P * t : 2 * P * (t + 1)].bitcast(FP4X4), b4_sc[:, a, P * t : P * (t + 1)]

        def d8_operand(a, nb):
            return d8_w[:, a, P * nb : P * (nb + 1)].bitcast(FP8X4), d8_sc[4 * a : P, P * nb : P * (nb + 1)]

        def group(passes):
            for i, (dst, (w, w_sc), (x, x_sc)) in enumerate(passes):
                nc.tensor.matmul_mx(out=dst, lhsT=w, lhsT_scale=w_sc, rhs=x, rhs_scale=x_sc,
                                    start=(i == 0), stop=(i == len(passes) - 1))

        def first_stage(name, first, count, bank_ids, weight, moving):
            per_bank = PACK // len(bank_ids)
            sums = []
            for u, b in enumerate(bank_ids):
                acc = bank("%s_%d_%d" % (name, first, u), b)
                dst = [acc[:, count * v : count * (v + 1)] for v in range(per_bank)]
                group([(dst[v], weight(a, per_bank * u + v), moving(a, first, count)) for a in range(PASSES) for v in range(per_bank)])
                sums.extend(dst)
            return sums

        west_sb, h_planes, h_bf = {}, {}, {}
        h_w = [sb("h_w%d" % half, [P, HALF], U32) for half in range(2)]
        h_sc = [sb("h_sc%d" % half, [P, HALF], U8) for half in range(2)]

        def west_stage(first, count, bank_ids):
            sums = first_stage("west", first, count, bank_ids, wa_operand, west_operand)
            west_sb[first] = sb("west_sb%d" % first, [P, PACK, count], F32)
            for t in range(PACK):
                nc.scalar.activation(west_sb[first][:, t, :], sums[t], ACT.Identity, bias=bw_t[:, t : t + 1])

        def east_stage(first, count, bank_ids, tag=None):
            sums = first_stage("east", first, count, bank_ids, b4_operand, east_operand)
            h_planes[first] = sb("h_planes%d" % first, [P, PACK, count], BF16, tag)
            for t in range(PACK):
                nc.vector.scalar_tensor_tensor(
                    h_planes[first][:, t, :], sums[t], be_t[:, t : t + 1], west_sb[first][:, t, :], ALU.add, ALU.max
                )

        def weave(first, count):
            h_bf[first] = sb("h_bf%d" % first, [P, PACK * count], BF16)
            nc.scalar.copy(
                h_bf[first][:].rearrange("p (n t) -> p n t", t=PACK),
                h_planes[first][:].rearrange("p t n -> p n t"),
            )

        def quantise_h(first, count):
            cols = slice(first % HALF, first % HALF + count)
            nc.vector.quantize_mx(out=h_w[first // HALF][:, cols].bitcast(FP8X4), scales=h_sc[first // HALF][:, cols], in_=h_bf[first][:])

        wc_w, wc_sc = {}, {}

        def quantise_wc(u):
            wc_bf = sb("wc_bf%d" % u, [P, PACK * 2 * P], BF16)
            wc_w[u] = sb("wc_w%d" % u, [P, 2 * P], U32)
            wc_sc[u] = sb("wc_sc%d" % u, [P, 2 * P], U8)
            nc.scalar.copy(
                wc_bf[:].rearrange("p (c j) -> p c j", j=PACK),
                wc_raw[:, :, 2 * P * u : 2 * P * (u + 1)].rearrange("p j c -> p c j"),
            )
            nc.vector.quantize_mx(out=wc_w[u][:].bitcast(FP8X4), scales=wc_sc[u][:], in_=wc_bf[:])

        def wc_operand(nb):
            cols = slice(P * (nb % 2), P * (nb % 2 + 1))
            return wc_w[nb // 2][:, cols].bitcast(FP8X4), wc_sc[nb // 2][:, cols]

        y = {}

        def second_stage(first, count, blocks, b, tags=None):
            acc = bank("y_%d_%d" % (first, blocks[0]), b)
            dst = [acc[:, count * v : count * (v + 1)] for v in range(len(blocks))]
            cols = slice(first % HALF, first % HALF + count)
            h_operand = (h_w[first // HALF][:, cols].bitcast(FP8X4), h_sc[first // HALF][:, cols])
            group(
                [(dst[v], d8_operand(a, nb), west_operand(a, first, count)) for v, nb in enumerate(blocks) for a in range(PASSES)]
                + [(dst[v], wc_operand(nb), h_operand) for v, nb in enumerate(blocks)]
            )
            for v, nb in enumerate(blocks):
                y[first, nb] = sb("y_sb_%d_%d" % (first, nb), [P, count], F32, tags)
                nc.scalar.activation(y[first, nb][:], dst[v], ACT.Tanh, bias=bo_t[:, nb : nb + 1])

        def place(first, count, nb):
            nc.vector.tensor_tensor(
                pages[nb][:].indirect(list_cols(place_list, first, count)),
                y[first, nb][:], wgo_t[:, first : first + count], ALU.mult,
            )

        def store(nb):
            nc.sync.dma_start(out[P * nb : P * (nb + 1), :], pages[nb][:])

        gather_pass1(west_w1, "west_w1_", west_list, 0)
        gather_pass1(east_w1, "east_w1_", east_list, 0)
        gather_pass1(west_w1, "west_w1_", west_list, 1)
        west_stage(0, CHUNK, (0, 1))
        east_stage(0, CHUNK, (2, 3))
        weave(0, CHUNK)
        quantise_h(0, CHUNK)
        quantise_wc(0)
        west_stage(CHUNK, CHUNK, (4, 5))
        second_stage(0, CHUNK, (0, 1), 0)
        gather_pass1(east_w1, "east_w1_", east_list, 1, "west_sb0")
        east_stage(CHUNK, CHUNK, (6, 7), "h_bf0")
        weave(CHUNK, CHUNK)
        quantise_h(CHUNK, CHUNK)
        west_stage(HALF, HALF, (1, 4, 5, 2))
        quantise_wc(1)
        east_stage(HALF, HALF, (3, 6, 7, 0))
        second_stage(CHUNK, CHUNK, (0, 1), 1)
        weave(HALF, HALF)
        quantise_h(HALF, HALF)
        second_stage(0, HALF, (2,), 4)
        second_stage(0, HALF, (3,), 5, "h_planes%d" % HALF)
        place(0, CHUNK, 0)
        place(0, CHUNK, 1)
        place(CHUNK, CHUNK, 0)
        place(CHUNK, CHUNK, 1)
        place(0, HALF, 2)
        place(0, HALF, 3)
        for nb, b in enumerate((2, 3, 6, 7)):
            second_stage(HALF, HALF, (nb,), b)
            place(HALF, HALF, nb)
            store(nb)
